import numpy as np
import ml_dtypes


def mxq(x, axis, fmt="e4m3"):
    dtype, down = {"e4m3": (ml_dtypes.float8_e4m3fn, 7), "e5m2": (ml_dtypes.float8_e5m2, 14)}[fmt]
    v = np.moveaxis(np.asarray(x, np.float32).astype(ml_dtypes.bfloat16).astype(np.float64), axis, -1)
    blocks = v.reshape(v.shape[:-1] + (-1, 32))
    amax = np.abs(blocks).max(-1, keepdims=True)
    byte = np.maximum(np.where(amax > 0, np.frexp(amax)[1] - 1 + 127, 0) - down, 1)
    scale = np.exp2(byte - 127.0)
    codes = (blocks / scale).astype(np.float32).astype(dtype).astype(np.float64)
    return np.moveaxis((codes * scale).reshape(v.shape), -1, axis)


WIDE = False


def mx_kscale(k):
    if not WIDE:
        return np.ones(k)
    levels = np.array([10, -10, 5, -5, 0])
    if k % 512:
        return np.exp2(np.random.permutation(np.resize(levels, k // 32))).repeat(32)
    a = np.empty((k // 512, 16))
    for p in range(k // 512):
        a[p, :8] = np.random.permutation(np.resize(levels, 8))
        for g in range(8):
            far = levels[np.abs(levels - a[p, g]) >= 10]
            a[p, g + 8] = far[np.random.randint(len(far))]
    return np.exp2(a.ravel()).repeat(32)


def f64(x):
    return np.asarray(x).astype(np.float64)


def striped(idx):
    return np.tile(idx.reshape(-1, 16).T, (8, 1)).astype(np.uint16)


def unstriped(offs):
    return offs[:16].T.reshape(-1).astype(np.int64)


def striped8(idx):
    return np.concatenate([x.reshape(-1, 16).T for x in idx]).astype(np.uint16)


def runs(offs, k):
    lists = np.stack([offs[16 * r : 16 * r + 16].T.reshape(-1) for r in range(8)]).astype(np.int64)
    return lists[np.arange(k) % 512 // 64]


def pack_weight(w):
    k, n = w.shape
    w = f64(np.asarray(w, np.float32).astype(ml_dtypes.bfloat16)).reshape(k // 32, 32, n)
    amax = np.abs(w).max(1)
    byte = np.clip(np.where(amax > 0, np.frexp(amax)[1] - 1 + 127 - 7, 1), 1, 254)
    scaled = (w * np.exp2(127.0 - byte)[:, None, :]).reshape(k, n).astype(np.float32)
    words = np.ascontiguousarray(scaled.reshape(k // 512, 128, 4, n).transpose(0, 1, 3, 2)).astype(ml_dtypes.float8_e4m3fn).view(np.uint8)
    return words, np.ascontiguousarray(byte.astype(np.uint8).reshape(k // 512, 16, n))


def unpack_weight(words, scales):
    g, p, n, _ = words.shape
    vals = np.ascontiguousarray(words).view(ml_dtypes.float8_e4m3fn).astype(np.float64) * np.repeat(np.exp2(scales.astype(np.float64) - 127.0), 8, axis=1)[..., None]
    return vals.transpose(0, 1, 3, 2).reshape(g * 512, n)


E2M1 = np.array([0.0, 0.5, 1.0, 1.5, 2.0, 3.0, 4.0, 6.0, -0.0, -0.5, -1.0, -1.5, -2.0, -3.0, -4.0, -6.0])


def pack_fp4(w):
    k, n = w.shape
    w = f64(np.asarray(w, np.float32).astype(ml_dtypes.bfloat16)).reshape(k // 32, 32, n)
    amax = np.abs(w).max(1)
    mant, ex = np.frexp(amax / 6.0)
    byte = np.clip(np.where(amax > 0, np.where(mant > 0.5, ex, ex - 1) + 127, 1), 1, 254)
    scaled = (w * np.exp2(127.0 - byte)[:, None, :]).reshape(k, n).astype(np.float32)
    c = np.ascontiguousarray(scaled.reshape(k // 512, 128, 4, n).transpose(0, 1, 3, 2)).astype(ml_dtypes.float4_e2m1fn).view(np.uint8) & 0xF
    words = (c[..., 0::2] | (c[..., 1::2] << 4)).reshape(k // 512, 128, 2 * n)
    return np.ascontiguousarray(words), np.ascontiguousarray(byte.astype(np.uint8).reshape(k // 512, 16, n))


def unpack_fp4(words, scales):
    g, _, n = scales.shape
    words = np.ascontiguousarray(words).reshape(g, 128, n, 2)
    nib = np.empty((g, 128, n, 4), np.uint8)
    nib[..., 0::2] = words & 0xF
    nib[..., 1::2] = words >> 4
    vals = E2M1[nib] * np.repeat(np.exp2(scales.astype(np.float64) - 127.0), 8, axis=1)[..., None]
    return vals.transpose(0, 1, 3, 2).reshape(g * 512, n)


def sigmoid(v):
    return 1.0 / (1.0 + np.exp(-np.maximum(v, -700.0)))

def planes(y):
    n, m = y.shape
    v = y.astype(np.float32).astype(ml_dtypes.bfloat16).astype(np.float64).reshape(n // 32, 32, m)
    top = np.abs(v).max(1)
    byte = np.clip(np.where(top > 0, np.frexp(top)[1] - 1 + 127 - 7, 1), 1, 254)
    codes = (v * np.exp2(127.0 - byte)[:, None, :]).reshape(n, m).astype(np.float32).astype(ml_dtypes.float8_e4m3fn).view(np.uint8)
    words = codes.reshape(n // 512, 128, 4, m).transpose(0, 1, 3, 2)
    return np.ascontiguousarray(words), np.ascontiguousarray(byte.astype(np.uint8).reshape(n // 512, 16, m))


K, T, S, H, C = 512, 2048, 512, 512, 512


def setup_inputs():
    n = np.random.standard_normal
    s = mx_kscale(K)[:, None]
    packed_xT = pack_weight(n((K, T)) * s)
    packed_w1 = pack_fp4(n((K, H)) / np.sqrt(K) / s)
    packed_w2 = pack_fp4(n((K, H)) / np.sqrt(K) / s)
    return {
        "x_words": packed_xT[0],
        "x_scales": packed_xT[1],
        "w1_words": packed_w1[0],
        "w1_scales": packed_w1[1],
        "w2_words": packed_w2[0],
        "w2_scales": packed_w2[1],
        "gs": (np.random.uniform(0.5, 1.5, (K, 1)) / s).astype(np.float32),
        "offs": striped(np.random.permutation(T)[:S]),
        "two": striped(np.random.permutation(T)[:S]),
        "n1": striped8(np.stack([np.random.permutation(S) for _ in range(8)])),
        "n2": striped8(np.stack([np.random.permutation(S) for _ in range(8)])),
        "cand": striped(np.random.permutation(T)[:C]),
        "n3": striped8(np.stack([np.random.permutation(S) for _ in range(8)])),
        "n4": striped8(np.stack([np.random.permutation(S) for _ in range(8)])),
    }


def reference(x_words, x_scales, w1_words, w1_scales, w2_words, w2_scales, gs, offs, two, n1, n2, cand, n3, n4):
    x_cand = unpack_weight(x_words, x_scales)[:, unstriped(cand)]
    xq = unpack_weight(x_words, x_scales)[:, unstriped(offs)]
    y = unpack_fp4(w1_words, w1_scales).T @ xq
    x_two = unpack_weight(x_words, x_scales)[:, unstriped(two)]
    d = unpack_fp4(w2_words, w2_scales).T @ x_two
    z = f64(gs) * (y * (sigmoid(d[np.arange(H)[:, None], runs(n2, H)])) - (0.5 * (y[np.arange(H)[:, None], runs(n1, H)])))
    s = 0.0625 * ((x_cand.T @ mxq(z, 0, "e4m3")))
    ex = np.exp(s)
    out_0 = np.log(ex + ex[np.arange(C)[:, None], runs(n3, C)]) - (s[np.arange(C)[:, None], runs(n4, C)])
    return (out_0,) + planes(out_0)

@@ -1,0 +1,228 @@
+from contextlib import ExitStack
+
+import concourse.mybir as mybir
+
+F32 = mybir.dt.float32
+BF16 = mybir.dt.bfloat16
+I32 = mybir.dt.int32
+U32 = mybir.dt.uint32
+U16 = mybir.dt.uint16
+U8 = mybir.dt.uint8
+FP8X4 = mybir.dt.float8_e4m3fn_x4
+FP4X4 = mybir.dt.float4_e2m1fn_x4
+ACT = mybir.ActivationFunctionType
+ALU = mybir.AluOpType
+
+P = 128
+R = 4
+T = 2048
+S = 512
+HALF = 256
+FLOPS = 3 * 2 * 512 * 512 * 512
+
+
+def tile_picked_twcgateblse_none_po_kernel(
+    tc, x_words, x_scales, w1_words, w1_scales, w2_words, w2_scales, gs, offs, two, n1, n2, cand, n3, n4, out_0, out_1, out_2
+):
+    nc = tc.nc
+    with ExitStack() as ctx:
+        lists = ctx.enter_context(tc.tile_pool(name="lists", bufs=1))
+        keep = ctx.enter_context(tc.tile_pool(name="keep", bufs=1))
+        psum = ctx.enter_context(tc.psum_pool(name="psum", bufs=1))
+
+        def sb(name, shape, dtype):
+            return keep.tile(shape, dtype, name=name, align_bytes=64)
+
+        def load_list(name, src):
+            tile = lists.tile([P, S // 16], U16, name=name)
+            nc.sync.dma_start(tile[:], src)
+            return tile
+
+        def load_scales(engine, tile, src):
+            for q in range(4):
+                engine.dma_start(tile[32 * q : 32 * q + 4, :].bitcast(I32), src[0, 4 * q : 4 * q + 4, :].bitcast(I32))
+
+        def half(h):
+            return slice(h * HALF, (h + 1) * HALF)
+
+        def offsets(lst, h):
+            return lst[:, h * HALF // 16 : (h + 1) * HALF // 16]
+
+        xw = sb("xw", [P, T], U32)
+        xs = sb("xs", [P, T], U8)
+        w_raw = [sb("w%d_raw" % i, [P, 2 * S], U8) for i in range(2)]
+        ws_raw = [sb("ws%d_raw" % i, [P, S], U8) for i in range(2)]
+        w_dealt = [sb("w%d_dealt" % i, [P, 2 * S], U8) for i in range(2)]
+        ws_dealt = [sb("ws%d_dealt" % i, [P, S], U8) for i in range(2)]
+        gain = sb("gain", [P, R], F32)
+
+        nc.gpsimd.memset(xs[:].bitcast(I32), 0)
+        nc.gpsimd.memset(ws_raw[0][:].bitcast(I32), 0)
+        nc.gpsimd.memset(ws_raw[1][:].bitcast(I32), 0)
+
+        x_rows = x_words[0].rearrange("p c r -> p (c r)").bitcast(I32)
+        nc.sync.dma_start(xw[:, : T // 2].bitcast(I32), x_rows[:, : T // 2])
+        offs_l = load_list("offs_l", offs)
+        load_scales(nc.sync, xs, x_scales)
+        nc.sync.dma_start(xw[:, T // 2 :].bitcast(I32), x_rows[:, T // 2 :])
+        nc.sync.dma_start(w_raw[0][:].bitcast(I32), w1_words[0].bitcast(I32))
+        load_scales(nc.sync, ws_raw[0], w1_scales)
+        two_l = load_list("two_l", two)
+        nc.sync.dma_start(gain[:], gs.rearrange("(p t) o -> p (t o)", t=R))
+        load_scales(nc.gpsimd, ws_raw[1], w2_scales)
+        n1_l = load_list("n1_l", n1)
+        nc.sync.dma_start(w_raw[1][:].bitcast(I32), w2_words[0].bitcast(I32))
+        cand_l = load_list("cand_l", cand)
+        n2_l = load_list("n2_l", n2)
+        n3_l = load_list("n3_l", n3)
+        n4_l = load_list("n4_l", n4)
+
+        def deal(ap):
+            return ap.rearrange("p (m t) -> p t m", t=R)
+
+        def dealt(ap):
+            return ap.rearrange("p (t m) -> p t m", t=R)
+
+        def gather_scales(name, lst):
+            tile = sb(name, [P, S], U8)
+            nc.vector.tensor_copy(tile[:], xs[:].indirect(lst[:]))
+            return tile
+
+        def gather_words(name, lst):
+            tile = sb(name, [P, S], U32)
+            nc.vector.tensor_copy(tile[:], xw[:].indirect(lst[:]))
+            return tile
+
+        for i in range(2):
+            nc.scalar.copy(dealt(w_dealt[i][:].bitcast(U16)), deal(w_raw[i][:].bitcast(U16)))
+        offs_s = gather_scales("offs_s", offs_l)
+        nc.vector.tensor_copy(dealt(ws_dealt[0][:]), deal(ws_raw[0][:]))
+        offs_w = gather_words("offs_w", offs_l)
+        nc.gpsimd.tensor_copy(dealt(ws_dealt[1][:]), deal(ws_raw[1][:]))
+        two_s = gather_scales("two_s", two_l)
+        two_w = gather_words("two_w", two_l)
+        cand_s = gather_scales("cand_s", cand_l)
+        cand_w = gather_words("cand_w", cand_l)
+        cand_sd = sb("cand_sd", [P, S], U8)
+        cand_wd = sb("cand_wd", [P, S], U32)
+        nc.vector.tensor_copy(dealt(cand_sd[:]), deal(cand_s[:]))
+        nc.vector.tensor_copy(dealt(cand_wd[:]), deal(cand_w[:]))
+
+        def project(i, t, words, scales):
+            bank = psum.tile([P, S], F32, name="bank%d" % (R * i + t))
+            nc.tensor.matmul_mx(
+                bank[:],
+                lhsT=w_dealt[i][:, 2 * P * t : 2 * P * (t + 1)].bitcast(FP4X4),
+                lhsT_scale=ws_dealt[i][:, P * t : P * (t + 1)],
+                rhs=words[:].bitcast(FP8X4),
+                rhs_scale=scales[:],
+                start=True,
+                stop=True,
+            )
+            return bank
+
+        y_bank = [project(0, t, offs_w, offs_s) for t in range(R)]
+        d_bank = [project(1, t, two_w, two_s) for t in range(R)]
+
+        gy = [sb("gy%d" % t, [P, S], F32) for t in range(R)]
+        sig = [sb("sig%d" % t, [P, S], F32) for t in range(R)]
+        gated = [sb("gated%d" % h, [P, R, HALF], F32) for h in range(2)]
+        pulled = [sb("pulled%d" % h, [P, R, HALF], F32) for h in range(2)]
+
+        def scale_y(t):
+            nc.scalar.activation(gy[t][:], y_bank[t][:], ACT.Copy, scale=gain[:, t : t + 1])
+
+        def squash_d(t):
+            nc.scalar.activation(sig[t][:], d_bank[t][:], ACT.Sigmoid)
+
+        def pull(t, h):
+            nc.scalar.activation(pulled[h][:, t, :], gy[t][:].indirect(offsets(n1_l, h)), ACT.Copy, scale=-0.5)
+
+        scale_y(0)
+        pull(0, 0)
+        scale_y(1)
+        pull(1, 0)
+        squash_d(0)
+        scale_y(2)
+        squash_d(1)
+        scale_y(3)
+        squash_d(2)
+        squash_d(3)
+        pull(2, 0)
+        pull(3, 0)
+        for t in range(R):
+            pull(t, 1)
+
+        def woven(ap):
+            return ap.rearrange("p (c i t) -> p c t i", i=4, t=R)
+
+        def weave(ap):
+            return ap.rearrange("p t (c i) -> p c t i", i=4)
+
+        s_bank = {}
+        for h in range(2):
+            for t in range(R):
+                nc.vector.tensor_tensor(gated[h][:, t, :], sig[t][:].indirect(offsets(n2_l, h)), gy[t][:, half(h)], ALU.mult)
+            z16 = sb("z16_%d" % h, [P, HALF * R], BF16)
+            nc.vector.tensor_tensor(woven(z16[:]), weave(gated[h][:]), weave(pulled[h][:]), ALU.add)
+            z_w = sb("z_w%d" % h, [P, HALF], U32)
+            z_s = sb("z_s%d" % h, [P, HALF], U8)
+            nc.vector.quantize_mx(z_w[:].bitcast(FP8X4), z_s[:], z16[:])
+            for t in range(R):
+                bank = psum.tile([P, HALF], F32, name="bank%d" % (R * h + t))
+                nc.tensor.matmul_mx(
+                    bank[:],
+                    lhsT=cand_wd[:, P * t : P * (t + 1)].bitcast(FP8X4),
+                    lhsT_scale=cand_sd[:, P * t : P * (t + 1)],
+                    rhs=z_w[:].bitcast(FP8X4),
+                    rhs_scale=z_s[:],
+                    start=True,
+                    stop=True,
+                )
+                s_bank[t, h] = bank
+
+        ex = [sb("ex%d" % t, [P, S], F32) for t in range(R)]
+        en = [sb("en%d" % t, [P, S], F32) for t in range(R)]
+        for t in range(R):
+            for h in range(2):
+                nc.scalar.activation(ex[t][:, half(h)], s_bank[t, h][:], ACT.Exp, scale=0.0625)
+            for h in range(2):
+                nc.scalar.activation(en[t][:, half(h)], s_bank[t, h][:], ACT.Exp, scale=-0.0625)
+
+        ON_VECTOR = 2
+        ex_copy = [sb("ex_copy%d" % t, [P, S], F32) for t in range(ON_VECTOR)]
+        fetched = [sb("fetched%d" % h, [P, R - ON_VECTOR, HALF], F32) for h in range(2)]
+        for h in range(2):
+            for t in range(ON_VECTOR, R):
+                nc.scalar.activation(fetched[h][:, t - ON_VECTOR, :], ex[t][:].indirect(offsets(n3_l, h)), ACT.Copy)
+
+        out_rows = out_0.rearrange("(p t) c -> p t c", t=R)
+        out_words = out_1[0].rearrange("p c r -> p (c r)").bitcast(I32)
+        o_s = sb("o_s", [P, S], U8)
+        for h in range(2):
+            total = sb("total%d" % h, [P, R, HALF], F32)
+            ratio = sb("ratio%d" % h, [P, R, HALF], F32)
+            for t in range(R):
+                if t < ON_VECTOR:
+                    if h == 0:
+                        nc.vector.tensor_copy(ex_copy[t][:], ex[t][:])
+                    nc.vector.tensor_tensor(total[:, t, :], ex[t][:].indirect(offsets(n3_l, h)), ex_copy[t][:, half(h)], ALU.add)
+                else:
+                    nc.vector.tensor_tensor(total[:, t, :], fetched[h][:, t - ON_VECTOR, :], ex[t][:, half(h)], ALU.add)
+                nc.vector.tensor_tensor(ratio[:, t, :], en[t][:].indirect(offsets(n4_l, h)), total[:, t, :], ALU.mult)
+            o32 = sb("o32_%d" % h, [P, R, HALF], F32)
+            o16 = sb("o16_%d" % h, [P, HALF * R], BF16)
+            if h == 0:
+                nc.scalar.activation(o32[:], ratio[:], ACT.Ln)
+                nc.scalar.copy(woven(o16[:]), weave(o32[:]))
+            else:
+                for t in range(R):
+                    nc.scalar.activation(o32[:, t, :], ratio[:, t, :], ACT.Ln)
+                nc.vector.tensor_copy(woven(o16[:]), weave(o32[:]))
+            nc.sync.dma_start(out_rows[:, :, half(h)], o32[:])
+            o_w = sb("o_w%d" % h, [P, HALF], U32)
+            nc.vector.quantize_mx(o_w[:].bitcast(FP8X4), o_s[:, half(h)], o16[:])
+            nc.sync.dma_start(out_words[:, half(h)], o_w[:].bitcast(I32))
+        for q in range(4):
+            engine = nc.sync if q % 2 else nc.scalar
+            engine.dma_start(out_2[0, 4 * q : 4 * q + 4, :].bitcast(I32), o_s[32 * q : 32 * q + 4, :].bitcast(I32))

@@ -30,49 +30,48 @@ def tile_picked_twcgateblse_none_po_kernel(
         keep = ctx.enter_context(tc.tile_pool(name="keep", bufs=1))
         psum = ctx.enter_context(tc.psum_pool(name="psum", bufs=1))
 
-        def sb(name, shape, dtype):
-            return keep.tile(shape, dtype, name=name, align_bytes=64)
+        def sb(name, shape, dtype, tag=None):
+            return keep.tile(shape, dtype, name=name, tag=tag or name, align_bytes=64)
 
         def load_list(name, src):
             tile = lists.tile([P, S // 16], U16, name=name)
             nc.sync.dma_start(tile[:], src)
             return tile
 
-        def load_scales(engine, tile, src):
+        def load_scales(tile, src):
             for q in range(4):
-                engine.dma_start(tile[32 * q : 32 * q + 4, :].bitcast(I32), src[0, 4 * q : 4 * q + 4, :].bitcast(I32))
+                nc.sync.dma_start(tile[32 * q : 32 * q + 4, :].bitcast(I32), src[0, 4 * q : 4 * q + 4, :].bitcast(I32))
 
         def half(h):
             return slice(h * HALF, (h + 1) * HALF)
 
-        def offsets(lst, h):
-            return lst[:, h * HALF // 16 : (h + 1) * HALF // 16]
+        def offsets(lst, cols):
+            return lst[:, cols.start // 16 : cols.stop // 16]
 
         xw = sb("xw", [P, T], U32)
         xs = sb("xs", [P, T], U8)
         w_raw = [sb("w%d_raw" % i, [P, 2 * S], U8) for i in range(2)]
         ws_raw = [sb("ws%d_raw" % i, [P, S], U8) for i in range(2)]
-        w_dealt = [sb("w%d_dealt" % i, [P, 2 * S], U8) for i in range(2)]
         ws_dealt = [sb("ws%d_dealt" % i, [P, S], U8) for i in range(2)]
         gain = sb("gain", [P, R], F32)
 
         nc.gpsimd.memset(xs[:].bitcast(I32), 0)
-        nc.gpsimd.memset(ws_raw[0][:].bitcast(I32), 0)
-        nc.gpsimd.memset(ws_raw[1][:].bitcast(I32), 0)
+        nc.vector.memset(ws_raw[1][:].bitcast(I32), 0)
+        nc.vector.memset(ws_raw[0][:].bitcast(I32), 0)
 
         x_rows = x_words[0].rearrange("p c r -> p (c r)").bitcast(I32)
         nc.sync.dma_start(xw[:, : T // 2].bitcast(I32), x_rows[:, : T // 2])
-        offs_l = load_list("offs_l", offs)
-        load_scales(nc.sync, xs, x_scales)
-        nc.sync.dma_start(xw[:, T // 2 :].bitcast(I32), x_rows[:, T // 2 :])
-        nc.sync.dma_start(w_raw[0][:].bitcast(I32), w1_words[0].bitcast(I32))
-        load_scales(nc.sync, ws_raw[0], w1_scales)
         two_l = load_list("two_l", two)
-        nc.sync.dma_start(gain[:], gs.rearrange("(p t) o -> p (t o)", t=R))
-        load_scales(nc.gpsimd, ws_raw[1], w2_scales)
-        n1_l = load_list("n1_l", n1)
+        load_scales(xs, x_scales)
+        nc.sync.dma_start(xw[:, T // 2 :].bitcast(I32), x_rows[:, T // 2 :])
         nc.sync.dma_start(w_raw[1][:].bitcast(I32), w2_words[0].bitcast(I32))
+        load_scales(ws_raw[1], w2_scales)
+        offs_l = load_list("offs_l", offs)
+        nc.sync.dma_start(w_raw[0][:].bitcast(I32), w1_words[0].bitcast(I32))
+        nc.sync.dma_start(gain[:], gs.rearrange("(p t) o -> p (t o)", t=R))
+        load_scales(ws_raw[0], w1_scales)
         cand_l = load_list("cand_l", cand)
+        n1_l = load_list("n1_l", n1)
         n2_l = load_list("n2_l", n2)
         n3_l = load_list("n3_l", n3)
         n4_l = load_list("n4_l", n4)
@@ -88,31 +87,36 @@ def tile_picked_twcgateblse_none_po_kernel(
             nc.vector.tensor_copy(tile[:], xs[:].indirect(lst[:]))
             return tile
 
-        def gather_words(name, lst):
-            tile = sb(name, [P, S], U32)
+        def gather_words(name, lst, tag=None):
+            tile = sb(name, [P, S], U32, tag=tag)
             nc.vector.tensor_copy(tile[:], xw[:].indirect(lst[:]))
             return tile
 
-        for i in range(2):
-            nc.scalar.copy(dealt(w_dealt[i][:].bitcast(U16)), deal(w_raw[i][:].bitcast(U16)))
-        offs_s = gather_scales("offs_s", offs_l)
-        nc.vector.tensor_copy(dealt(ws_dealt[0][:]), deal(ws_raw[0][:]))
-        offs_w = gather_words("offs_w", offs_l)
-        nc.gpsimd.tensor_copy(dealt(ws_dealt[1][:]), deal(ws_raw[1][:]))
+        w2_first = sb("w2_first", [P, 2 * P], U8, tag="after_first_product")
+        w2_rest = sb("w2_rest", [P, 2 * (S - P)], U8)
+        w2_words16 = deal(w_raw[1][:].bitcast(U16))
+        nc.scalar.copy(w2_first[:].bitcast(U16), w2_words16[:, 0, :])
+        nc.scalar.copy(w2_rest[:].bitcast(U16).rearrange("p (t m) -> p t m", t=R - 1), w2_words16[:, 1:, :])
         two_s = gather_scales("two_s", two_l)
         two_w = gather_words("two_w", two_l)
+        nc.vector.tensor_copy(dealt(ws_dealt[1][:]), deal(ws_raw[1][:]))
+        offs_s = gather_scales("offs_s", offs_l)
+        offs_w = gather_words("offs_w", offs_l)
+        nc.vector.tensor_copy(dealt(ws_dealt[0][:]), deal(ws_raw[0][:]))
         cand_s = gather_scales("cand_s", cand_l)
         cand_w = gather_words("cand_w", cand_l)
         cand_sd = sb("cand_sd", [P, S], U8)
         cand_wd = sb("cand_wd", [P, S], U32)
         nc.vector.tensor_copy(dealt(cand_sd[:]), deal(cand_s[:]))
-        nc.vector.tensor_copy(dealt(cand_wd[:]), deal(cand_w[:]))
+        nc.vector.tensor_copy(
+            cand_wd[:].rearrange("p (t c i) -> p c t i", t=R, i=4), cand_w[:].rearrange("p (c i t) -> p c t i", t=R, i=4)
+        )
 
-        def project(i, t, words, scales):
+        def project(i, t, weights, words, scales):
             bank = psum.tile([P, S], F32, name="bank%d" % (R * i + t))
             nc.tensor.matmul_mx(
                 bank[:],
-                lhsT=w_dealt[i][:, 2 * P * t : 2 * P * (t + 1)].bitcast(FP4X4),
+                lhsT=weights.bitcast(FP4X4),
                 lhsT_scale=ws_dealt[i][:, P * t : P * (t + 1)],
                 rhs=words[:].bitcast(FP8X4),
                 rhs_scale=scales[:],
@@ -121,13 +125,15 @@ def tile_picked_twcgateblse_none_po_kernel(
             )
             return bank
 
-        y_bank = [project(0, t, offs_w, offs_s) for t in range(R)]
-        d_bank = [project(1, t, two_w, two_s) for t in range(R)]
+        d_bank = [project(1, 0, w2_first[:], two_w, two_s)]
+        d_bank += [project(1, t, w2_rest[:, 2 * P * (t - 1) : 2 * P * t], two_w, two_s) for t in range(1, R)]
 
         gy = [sb("gy%d" % t, [P, S], F32) for t in range(R)]
         sig = [sb("sig%d" % t, [P, S], F32) for t in range(R)]
         gated = [sb("gated%d" % h, [P, R, HALF], F32) for h in range(2)]
         pulled = [sb("pulled%d" % h, [P, R, HALF], F32) for h in range(2)]
+
+        y_bank = []
 
         def scale_y(t):
             nc.scalar.activation(gy[t][:], y_bank[t][:], ACT.Copy, scale=gain[:, t : t + 1])
@@ -136,93 +142,156 @@ def tile_picked_twcgateblse_none_po_kernel(
             nc.scalar.activation(sig[t][:], d_bank[t][:], ACT.Sigmoid)
 
         def pull(t, h):
-            nc.scalar.activation(pulled[h][:, t, :], gy[t][:].indirect(offsets(n1_l, h)), ACT.Copy, scale=-0.5)
+            nc.scalar.activation(pulled[h][:, t, :], gy[t][:].indirect(offsets(n1_l, half(h))), ACT.Copy, scale=-0.5)
 
-        scale_y(0)
-        pull(0, 0)
-        scale_y(1)
-        pull(1, 0)
         squash_d(0)
+        w1_dealt = sb("w1_dealt", [P, 2 * S], U8, tag="after_first_product")
+        nc.scalar.copy(dealt(w1_dealt[:].bitcast(U16)), deal(w_raw[0][:].bitcast(U16)))
+        y_bank.extend(project(0, t, w1_dealt[:, 2 * P * t : 2 * P * (t + 1)], offs_w, offs_s) for t in range(R))
+        for t in range(1, R):
+            squash_d(t)
+        scale_y(0)
+        scale_y(1)
+        pull(0, 0)
         scale_y(2)
-        squash_d(1)
+        pull(1, 0)
         scale_y(3)
-        squash_d(2)
-        squash_d(3)
         pull(2, 0)
         pull(3, 0)
         for t in range(R):
             pull(t, 1)
 
-        def woven(ap):
-            return ap.rearrange("p (c i t) -> p c t i", i=4, t=R)
+        def woven(ap, run):
+            return ap.rearrange("p (c i t) -> p c t i", i=run, t=R)
 
-        def weave(ap):
-            return ap.rearrange("p t (c i) -> p c t i", i=4)
+        def weave(ap, run):
+            return ap.rearrange("p t (c i) -> p c t i", i=run)
 
+        z16 = [sb("z16_%d" % h, [P, HALF * R], BF16) for h in range(2)]
+        z_w = [sb("z_w%d" % h, [P, HALF], U32) for h in range(2)]
+        z_s = [sb("z_s%d" % h, [P, HALF], U8) for h in range(2)]
         s_bank = {}
-        for h in range(2):
+
+        def gate(t, h):
+            nc.vector.tensor_tensor(gated[h][:, t, :], sig[t][:].indirect(offsets(n2_l, half(h))), gy[t][:, half(h)], ALU.mult)
+
+        def combine(h):
+            nc.vector.tensor_tensor(woven(z16[h][:], 2), weave(gated[h][:], 2), weave(pulled[h][:], 2), ALU.add)
+
+        def score(h):
+            nc.vector.quantize_mx(z_w[h][:].bitcast(FP8X4), z_s[h][:], z16[h][:])
             for t in range(R):
-                nc.vector.tensor_tensor(gated[h][:, t, :], sig[t][:].indirect(offsets(n2_l, h)), gy[t][:, half(h)], ALU.mult)
-            z16 = sb("z16_%d" % h, [P, HALF * R], BF16)
-            nc.vector.tensor_tensor(woven(z16[:]), weave(gated[h][:]), weave(pulled[h][:]), ALU.add)
-            z_w = sb("z_w%d" % h, [P, HALF], U32)
-            z_s = sb("z_s%d" % h, [P, HALF], U8)
-            nc.vector.quantize_mx(z_w[:].bitcast(FP8X4), z_s[:], z16[:])
-            for t in range(R):
-                bank = psum.tile([P, HALF], F32, name="bank%d" % (R * h + t))
+                bank = psum.tile([P, HALF], F32, name="bank%d" % (R * (1 - h) + t))
                 nc.tensor.matmul_mx(
                     bank[:],
                     lhsT=cand_wd[:, P * t : P * (t + 1)].bitcast(FP8X4),
                     lhsT_scale=cand_sd[:, P * t : P * (t + 1)],
-                    rhs=z_w[:].bitcast(FP8X4),
-                    rhs_scale=z_s[:],
+                    rhs=z_w[h][:].bitcast(FP8X4),
+                    rhs_scale=z_s[h][:],
                     start=True,
                     stop=True,
                 )
                 s_bank[t, h] = bank
 
-        ex = [sb("ex%d" % t, [P, S], F32) for t in range(R)]
-        en = [sb("en%d" % t, [P, S], F32) for t in range(R)]
         for t in range(R):
-            for h in range(2):
-                nc.scalar.activation(ex[t][:, half(h)], s_bank[t, h][:], ACT.Exp, scale=0.0625)
-            for h in range(2):
-                nc.scalar.activation(en[t][:, half(h)], s_bank[t, h][:], ACT.Exp, scale=-0.0625)
+            gate(t, 0)
+        gate(0, 1)
+        combine(0)
+        gate(1, 1)
+        score(0)
+        gate(2, 1)
+        gate(3, 1)
+        combine(1)
+        score(1)
 
         ON_VECTOR = 2
+        pieces = [slice(0, 256), slice(256, 384), slice(384, 512)]
+        widths = [cols.stop - cols.start for cols in pieces]
+        ex = [sb("ex%d" % t, [P, S], F32) for t in range(R)]
+        en = [sb("en%d" % t, [P, S], F32) for t in range(R)]
         ex_copy = [sb("ex_copy%d" % t, [P, S], F32) for t in range(ON_VECTOR)]
-        fetched = [sb("fetched%d" % h, [P, R - ON_VECTOR, HALF], F32) for h in range(2)]
-        for h in range(2):
-            for t in range(ON_VECTOR, R):
-                nc.scalar.activation(fetched[h][:, t - ON_VECTOR, :], ex[t][:].indirect(offsets(n3_l, h)), ACT.Copy)
+        fetched = [sb("fetched%d" % k, [P, R - ON_VECTOR, w], F32) for k, w in enumerate(widths)]
+        total = [sb("total%d" % k, [P, R, w], F32) for k, w in enumerate(widths)]
+        ratio = [sb("ratio%d" % k, [P, R, w], F32) for k, w in enumerate(widths)]
+        o32 = [sb("o32_%d" % k, [P, R, w], F32) for k, w in enumerate(widths)]
+        o16 = [sb("o16_%d" % k, [P, w * R], BF16) for k, w in enumerate(widths)]
+        o_w = [sb("o_w%d" % k, [P, w], U32) for k, w in enumerate(widths)]
+        o_s = sb("o_s", [P, S], U8)
+
+        def exp_up(t, h):
+            nc.scalar.activation(ex[t][:, half(h)], s_bank[t, h][:], ACT.Exp, scale=0.0625)
+            if t < ON_VECTOR:
+                if h == 0:
+                    nc.vector.tensor_copy(ex_copy[t][:, half(h)], ex[t][:, half(h)])
+                else:
+                    nc.sync.dma_start(ex_copy[t][:, half(h)], ex[t][:, half(h)])
+
+        def exp_down(t, h):
+            nc.scalar.activation(en[t][:, half(h)], s_bank[t, h][:], ACT.Exp, scale=-0.0625)
+
+        def fetch(t, k):
+            nc.scalar.activation(fetched[k][:, t - ON_VECTOR, :], ex[t][:].indirect(offsets(n3_l, pieces[k])), ACT.Copy)
+
+        def add_pair(t, k):
+            if t < ON_VECTOR:
+                nc.vector.tensor_tensor(total[k][:, t, :], ex[t][:].indirect(offsets(n3_l, pieces[k])), ex_copy[t][:, pieces[k]], ALU.add)
+            else:
+                nc.vector.tensor_tensor(total[k][:, t, :], fetched[k][:, t - ON_VECTOR, :], ex[t][:, pieces[k]], ALU.add)
+
+        def divide(t, k):
+            nc.vector.tensor_tensor(ratio[k][:, t, :], en[t][:].indirect(offsets(n4_l, pieces[k])), total[k][:, t, :], ALU.mult)
+
+        def ratios(k):
+            for t in (0, 2):
+                add_pair(t, k)
+                add_pair(t + 1, k)
+                divide(t, k)
+                divide(t + 1, k)
 
         out_rows = out_0.rearrange("(p t) c -> p t c", t=R)
         out_words = out_1[0].rearrange("p c r -> p (c r)").bitcast(I32)
-        o_s = sb("o_s", [P, S], U8)
-        for h in range(2):
-            total = sb("total%d" % h, [P, R, HALF], F32)
-            ratio = sb("ratio%d" % h, [P, R, HALF], F32)
-            for t in range(R):
-                if t < ON_VECTOR:
-                    if h == 0:
-                        nc.vector.tensor_copy(ex_copy[t][:], ex[t][:])
-                    nc.vector.tensor_tensor(total[:, t, :], ex[t][:].indirect(offsets(n3_l, h)), ex_copy[t][:, half(h)], ALU.add)
-                else:
-                    nc.vector.tensor_tensor(total[:, t, :], fetched[h][:, t - ON_VECTOR, :], ex[t][:, half(h)], ALU.add)
-                nc.vector.tensor_tensor(ratio[:, t, :], en[t][:].indirect(offsets(n4_l, h)), total[:, t, :], ALU.mult)
-            o32 = sb("o32_%d" % h, [P, R, HALF], F32)
-            o16 = sb("o16_%d" % h, [P, HALF * R], BF16)
-            if h == 0:
-                nc.scalar.activation(o32[:], ratio[:], ACT.Ln)
-                nc.scalar.copy(woven(o16[:]), weave(o32[:]))
-            else:
-                for t in range(R):
-                    nc.scalar.activation(o32[:, t, :], ratio[:, t, :], ACT.Ln)
-                nc.vector.tensor_copy(woven(o16[:]), weave(o32[:]))
-            nc.sync.dma_start(out_rows[:, :, half(h)], o32[:])
-            o_w = sb("o_w%d" % h, [P, HALF], U32)
-            nc.vector.quantize_mx(o_w[:].bitcast(FP8X4), o_s[:, half(h)], o16[:])
-            nc.sync.dma_start(out_words[:, half(h)], o_w[:].bitcast(I32))
+
+        def planes(k):
+            nc.vector.quantize_mx(o_w[k][:].bitcast(FP8X4), o_s[:, pieces[k]], o16[k][:])
+            nc.sync.dma_start(out_words[:, pieces[k]], o_w[k][:].bitcast(I32))
+
+        exp_up(0, 0)
+        exp_up(1, 0)
+        exp_up(0, 1)
+        exp_up(1, 1)
+        exp_down(0, 0)
+        exp_down(0, 1)
+        exp_up(2, 0)
+        exp_up(2, 1)
+        exp_down(1, 0)
+        exp_down(1, 1)
+        exp_up(3, 0)
+        exp_up(3, 1)
+        fetch(2, 0)
+        exp_down(2, 0)
+        exp_down(2, 1)
+        fetch(3, 0)
+        exp_down(3, 0)
+        exp_down(3, 1)
+
+        ratios(0)
+        nc.scalar.activation(o32[0][:], ratio[0][:], ACT.Ln)
+        nc.sync.dma_start(out_rows[:, :, pieces[0]], o32[0][:])
+        for k in (1, 2):
+            fetch(2, k)
+            fetch(3, k)
+        nc.scalar.copy(woven(o16[0][:], 2), weave(o32[0][:], 2))
+        ratios(1)
+        planes(0)
+        nc.scalar.activation(o32[1][:], ratio[1][:], ACT.Ln)
+        nc.sync.dma_start(out_rows[:, :, pieces[1]], o32[1][:])
+        ratios(2)
+        for t in (0, 2):
+            nc.scalar.activation(o32[2][:, t : t + 2, :], ratio[2][:, t : t + 2, :], ACT.Ln)
+        nc.sync.dma_start(out_rows[:, :, pieces[2]], o32[2][:])
+        for k in (1, 2):
+            nc.vector.tensor_copy(woven(o16[k][:], 2), weave(o32[k][:], 2))
+            planes(k)
         for q in range(4):
             engine = nc.sync if q % 2 else nc.scalar
             engine.dma_start(out_2[0, 4 * q : 4 * q + 4, :].bitcast(I32), o_s[32 * q : 32 * q + 4, :].bitcast(I32))

@@ -92,25 +92,19 @@ def tile_picked_twcgateblse_none_po_kernel(
             nc.vector.tensor_copy(tile[:], xw[:].indirect(lst[:]))
             return tile
 
-        w2_first = sb("w2_first", [P, 2 * P], U8, tag="after_first_product")
-        w2_rest = sb("w2_rest", [P, 2 * (S - P)], U8)
-        w2_words16 = deal(w_raw[1][:].bitcast(U16))
-        nc.scalar.copy(w2_first[:].bitcast(U16), w2_words16[:, 0, :])
-        nc.scalar.copy(w2_rest[:].bitcast(U16).rearrange("p (t m) -> p t m", t=R - 1), w2_words16[:, 1:, :])
+        w_dealt = [sb("w%d_dealt" % i, [P, 2 * S], U8) for i in range(2)]
+        for i in (1, 0):
+            nc.scalar.copy(dealt(w_dealt[i][:].bitcast(U16)), deal(w_raw[i][:].bitcast(U16)))
         two_s = gather_scales("two_s", two_l)
         two_w = gather_words("two_w", two_l)
         nc.vector.tensor_copy(dealt(ws_dealt[1][:]), deal(ws_raw[1][:]))
         offs_s = gather_scales("offs_s", offs_l)
         offs_w = gather_words("offs_w", offs_l)
         nc.vector.tensor_copy(dealt(ws_dealt[0][:]), deal(ws_raw[0][:]))
-        cand_s = gather_scales("cand_s", cand_l)
-        cand_w = gather_words("cand_w", cand_l)
         cand_sd = sb("cand_sd", [P, S], U8)
         cand_wd = sb("cand_wd", [P, S], U32)
-        nc.vector.tensor_copy(dealt(cand_sd[:]), deal(cand_s[:]))
-        nc.vector.tensor_copy(
-            cand_wd[:].rearrange("p (t c i) -> p c t i", t=R, i=4), cand_w[:].rearrange("p (c i t) -> p c t i", t=R, i=4)
-        )
+        nc.vector.tensor_copy(cand_sd[:].rearrange("p (t m) -> p m t", t=R), xs[:].indirect(cand_l[:]))
+        nc.vector.tensor_copy(cand_wd[:].rearrange("p (t m) -> p m t", t=R), xw[:].indirect(cand_l[:]))
 
         def project(i, t, weights, words, scales):
             bank = psum.tile([P, S], F32, name="bank%d" % (R * i + t))
@@ -125,30 +119,26 @@ def tile_picked_twcgateblse_none_po_kernel(
             )
             return bank
 
-        d_bank = [project(1, 0, w2_first[:], two_w, two_s)]
-        d_bank += [project(1, t, w2_rest[:, 2 * P * (t - 1) : 2 * P * t], two_w, two_s) for t in range(1, R)]
+        d_bank = [project(1, t, w_dealt[1][:, 2 * P * t : 2 * P * (t + 1)], two_w, two_s) for t in range(R)]
+        y_bank = [project(0, t, w_dealt[0][:, 2 * P * t : 2 * P * (t + 1)], offs_w, offs_s) for t in range(R)]
 
+        th = [sb("th%d" % t, [P, S], F32) for t in range(R)]
         gy = [sb("gy%d" % t, [P, S], F32) for t in range(R)]
         sig = [sb("sig%d" % t, [P, S], F32) for t in range(R)]
         gated = [sb("gated%d" % h, [P, R, HALF], F32) for h in range(2)]
         pulled = [sb("pulled%d" % h, [P, R, HALF], F32) for h in range(2)]
 
-        y_bank = []
-
         def scale_y(t):
             nc.scalar.activation(gy[t][:], y_bank[t][:], ACT.Copy, scale=gain[:, t : t + 1])
 
         def squash_d(t):
-            nc.scalar.activation(sig[t][:], d_bank[t][:], ACT.Sigmoid)
+            nc.scalar.activation(th[t][:], d_bank[t][:], ACT.Tanh, scale=0.5)
+            nc.gpsimd.tensor_scalar(sig[t][:], th[t][:], 0.5, 0.5, ALU.mult, ALU.add)
 
         def pull(t, h):
             nc.scalar.activation(pulled[h][:, t, :], gy[t][:].indirect(offsets(n1_l, half(h))), ACT.Copy, scale=-0.5)
 
-        squash_d(0)
-        w1_dealt = sb("w1_dealt", [P, 2 * S], U8, tag="after_first_product")
-        nc.scalar.copy(dealt(w1_dealt[:].bitcast(U16)), deal(w_raw[0][:].bitcast(U16)))
-        y_bank.extend(project(0, t, w1_dealt[:, 2 * P * t : 2 * P * (t + 1)], offs_w, offs_s) for t in range(R))
-        for t in range(1, R):
+        for t in range(R):
             squash_d(t)
         scale_y(0)
         scale_y(1)
@@ -167,7 +157,7 @@ def tile_picked_twcgateblse_none_po_kernel(
         def weave(ap, run):
             return ap.rearrange("p t (c i) -> p c t i", i=run)
 
-        z16 = [sb("z16_%d" % h, [P, HALF * R], BF16) for h in range(2)]
+        z16 = {}
         z_w = [sb("z_w%d" % h, [P, HALF], U32) for h in range(2)]
         z_s = [sb("z_s%d" % h, [P, HALF], U8) for h in range(2)]
         s_bank = {}
@@ -176,6 +166,7 @@ def tile_picked_twcgateblse_none_po_kernel(
             nc.vector.tensor_tensor(gated[h][:, t, :], sig[t][:].indirect(offsets(n2_l, half(h))), gy[t][:, half(h)], ALU.mult)
 
         def combine(h):
+            z16[h] = sb("z16", [P, HALF * R], BF16)
             nc.vector.tensor_tensor(woven(z16[h][:], 2), weave(gated[h][:], 2), weave(pulled[h][:], 2), ALU.add)
 
         def score(h):
@@ -210,8 +201,8 @@ def tile_picked_twcgateblse_none_po_kernel(
         ex = [sb("ex%d" % t, [P, S], F32) for t in range(R)]
         en = [sb("en%d" % t, [P, S], F32) for t in range(R)]
         ex_copy = [sb("ex_copy%d" % t, [P, S], F32) for t in range(ON_VECTOR)]
-        fetched = [sb("fetched%d" % k, [P, R - ON_VECTOR, w], F32) for k, w in enumerate(widths)]
-        total = [sb("total%d" % k, [P, R, w], F32) for k, w in enumerate(widths)]
+        fetched = [sb("fetched%d" % h, [P, R - ON_VECTOR, HALF], F32) for h in range(2)]
+        total = sb("total", [P, R, S], F32)
         ratio = [sb("ratio%d" % k, [P, R, w], F32) for k, w in enumerate(widths)]
         o32 = [sb("o32_%d" % k, [P, R, w], F32) for k, w in enumerate(widths)]
         o16 = [sb("o16_%d" % k, [P, w * R], BF16) for k, w in enumerate(widths)]
@@ -229,24 +220,17 @@ def tile_picked_twcgateblse_none_po_kernel(
         def exp_down(t, h):
             nc.scalar.activation(en[t][:, half(h)], s_bank[t, h][:], ACT.Exp, scale=-0.0625)
 
-        def fetch(t, k):
-            nc.scalar.activation(fetched[k][:, t - ON_VECTOR, :], ex[t][:].indirect(offsets(n3_l, pieces[k])), ACT.Copy)
+        def fetch(t, h):
+            nc.scalar.activation(fetched[h][:, t - ON_VECTOR, :], ex[t][:].indirect(offsets(n3_l, half(h))), ACT.Copy)
 
-        def add_pair(t, k):
+        def add_pair(t, h):
             if t < ON_VECTOR:
-                nc.vector.tensor_tensor(total[k][:, t, :], ex[t][:].indirect(offsets(n3_l, pieces[k])), ex_copy[t][:, pieces[k]], ALU.add)
+                nc.vector.tensor_tensor(total[:, t, half(h)], ex[t][:].indirect(offsets(n3_l, half(h))), ex_copy[t][:, half(h)], ALU.add)
             else:
-                nc.vector.tensor_tensor(total[k][:, t, :], fetched[k][:, t - ON_VECTOR, :], ex[t][:, pieces[k]], ALU.add)
+                nc.vector.tensor_tensor(total[:, t, half(h)], fetched[h][:, t - ON_VECTOR, :], ex[t][:, half(h)], ALU.add)
 
         def divide(t, k):
-            nc.vector.tensor_tensor(ratio[k][:, t, :], en[t][:].indirect(offsets(n4_l, pieces[k])), total[k][:, t, :], ALU.mult)
-
-        def ratios(k):
-            for t in (0, 2):
-                add_pair(t, k)
-                add_pair(t + 1, k)
-                divide(t, k)
-                divide(t + 1, k)
+            nc.vector.tensor_tensor(ratio[k][:, t, :], en[t][:].indirect(offsets(n4_l, pieces[k])), total[:, t, pieces[k]], ALU.mult)
 
         out_rows = out_0.rearrange("(p t) c -> p t c", t=R)
         out_words = out_1[0].rearrange("p c r -> p (c r)").bitcast(I32)
@@ -274,18 +258,26 @@ def tile_picked_twcgateblse_none_po_kernel(
         exp_down(3, 0)
         exp_down(3, 1)
 
-        ratios(0)
+        for t in (0, 2):
+            add_pair(t, 0)
+            add_pair(t + 1, 0)
+            divide(t, 0)
+            divide(t + 1, 0)
         nc.scalar.activation(o32[0][:], ratio[0][:], ACT.Ln)
         nc.sync.dma_start(out_rows[:, :, pieces[0]], o32[0][:])
-        for k in (1, 2):
-            fetch(2, k)
-            fetch(3, k)
+        fetch(2, 1)
+        fetch(3, 1)
         nc.scalar.copy(woven(o16[0][:], 2), weave(o32[0][:], 2))
-        ratios(1)
+        for t in (0, 2):
+            add_pair(t, 1)
+            add_pair(t + 1, 1)
+            divide(t, 1)
+            divide(t + 1, 1)
         planes(0)
         nc.scalar.activation(o32[1][:], ratio[1][:], ACT.Ln)
         nc.sync.dma_start(out_rows[:, :, pieces[1]], o32[1][:])
-        ratios(2)
+        for t in range(R):
+            divide(t, 2)
         for t in (0, 2):
             nc.scalar.activation(o32[2][:, t : t + 2, :], ratio[2][:, t : t + 2, :], ACT.Ln)
         nc.sync.dma_start(out_rows[:, :, pieces[2]], o32[2][:])

@@ -17,7 +17,10 @@ P = 128
 R = 4
 T = 2048
 S = 512
-HALF = 256
+HALF = S // 2
+QUADRANTS = 4
+ON_VECTOR = 2
+PIECES = [slice(0, 256), slice(256, 384), slice(384, 512)]
 FLOPS = 3 * 2 * 512 * 512 * 512
 
 
@@ -30,8 +33,8 @@ def tile_picked_twcgateblse_none_po_kernel(
         keep = ctx.enter_context(tc.tile_pool(name="keep", bufs=1))
         psum = ctx.enter_context(tc.psum_pool(name="psum", bufs=1))
 
-        def sb(name, shape, dtype, tag=None):
-            return keep.tile(shape, dtype, name=name, tag=tag or name, align_bytes=64)
+        def sb(name, shape, dtype):
+            return keep.tile(shape, dtype, name=name, align_bytes=64)
 
         def load_list(name, src):
             tile = lists.tile([P, S // 16], U16, name=name)
@@ -39,7 +42,7 @@ def tile_picked_twcgateblse_none_po_kernel(
             return tile
 
         def load_scales(tile, src):
-            for q in range(4):
+            for q in range(QUADRANTS):
                 nc.sync.dma_start(tile[32 * q : 32 * q + 4, :].bitcast(I32), src[0, 4 * q : 4 * q + 4, :].bitcast(I32))
 
         def half(h):
@@ -55,21 +58,21 @@ def tile_picked_twcgateblse_none_po_kernel(
         ws_dealt = [sb("ws%d_dealt" % i, [P, S], U8) for i in range(2)]
         gain = sb("gain", [P, R], F32)
 
-        nc.gpsimd.memset(xs[:].bitcast(I32), 0)
+        nc.vector.memset(xs[:].bitcast(I32), 0)
         nc.vector.memset(ws_raw[1][:].bitcast(I32), 0)
         nc.vector.memset(ws_raw[0][:].bitcast(I32), 0)
 
+        for i, words in ((1, w2_words), (0, w1_words)):
+            nc.gpsimd.dma_start(w_raw[i][:].bitcast(I32), words[0].bitcast(I32))
         x_rows = x_words[0].rearrange("p c r -> p (c r)").bitcast(I32)
         nc.sync.dma_start(xw[:, : T // 2].bitcast(I32), x_rows[:, : T // 2])
         two_l = load_list("two_l", two)
         load_scales(xs, x_scales)
         nc.sync.dma_start(xw[:, T // 2 :].bitcast(I32), x_rows[:, T // 2 :])
-        nc.sync.dma_start(w_raw[1][:].bitcast(I32), w2_words[0].bitcast(I32))
         load_scales(ws_raw[1], w2_scales)
         offs_l = load_list("offs_l", offs)
-        nc.sync.dma_start(w_raw[0][:].bitcast(I32), w1_words[0].bitcast(I32))
-        nc.sync.dma_start(gain[:], gs.rearrange("(p t) o -> p (t o)", t=R))
         load_scales(ws_raw[0], w1_scales)
+        nc.sync.dma_start(gain[:], gs.rearrange("(p t) o -> p (t o)", t=R))
         cand_l = load_list("cand_l", cand)
         n1_l = load_list("n1_l", n1)
         n2_l = load_list("n2_l", n2)
@@ -87,8 +90,8 @@ def tile_picked_twcgateblse_none_po_kernel(
             nc.vector.tensor_copy(tile[:], xs[:].indirect(lst[:]))
             return tile
 
-        def gather_words(name, lst, tag=None):
-            tile = sb(name, [P, S], U32, tag=tag)
+        def gather_words(name, lst):
+            tile = sb(name, [P, S], U32)
             nc.vector.tensor_copy(tile[:], xw[:].indirect(lst[:]))
             return tile
 
@@ -101,16 +104,16 @@ def tile_picked_twcgateblse_none_po_kernel(
         offs_s = gather_scales("offs_s", offs_l)
         offs_w = gather_words("offs_w", offs_l)
         nc.vector.tensor_copy(dealt(ws_dealt[0][:]), deal(ws_raw[0][:]))
-        cand_sd = sb("cand_sd", [P, S], U8)
-        cand_wd = sb("cand_wd", [P, S], U32)
-        nc.vector.tensor_copy(cand_sd[:].rearrange("p (t m) -> p m t", t=R), xs[:].indirect(cand_l[:]))
-        nc.vector.tensor_copy(cand_wd[:].rearrange("p (t m) -> p m t", t=R), xw[:].indirect(cand_l[:]))
+        cand_s = sb("cand_s", [P, S], U8)
+        cand_w = sb("cand_w", [P, S], U32)
+        nc.vector.tensor_copy(cand_s[:].rearrange("p (t m) -> p m t", t=R), xs[:].indirect(cand_l[:]))
+        nc.vector.tensor_copy(cand_w[:].rearrange("p (t m) -> p m t", t=R), xw[:].indirect(cand_l[:]))
 
-        def project(i, t, weights, words, scales):
+        def project(i, t, words, scales):
             bank = psum.tile([P, S], F32, name="bank%d" % (R * i + t))
             nc.tensor.matmul_mx(
                 bank[:],
-                lhsT=weights.bitcast(FP4X4),
+                lhsT=w_dealt[i][:, 2 * P * t : 2 * P * (t + 1)].bitcast(FP4X4),
                 lhsT_scale=ws_dealt[i][:, P * t : P * (t + 1)],
                 rhs=words[:].bitcast(FP8X4),
                 rhs_scale=scales[:],
@@ -119,43 +122,32 @@ def tile_picked_twcgateblse_none_po_kernel(
             )
             return bank
 
-        d_bank = [project(1, t, w_dealt[1][:, 2 * P * t : 2 * P * (t + 1)], two_w, two_s) for t in range(R)]
-        y_bank = [project(0, t, w_dealt[0][:, 2 * P * t : 2 * P * (t + 1)], offs_w, offs_s) for t in range(R)]
+        d_bank = [project(1, t, two_w, two_s) for t in range(R)]
+        y_bank = [project(0, t, offs_w, offs_s) for t in range(R)]
 
-        th = [sb("th%d" % t, [P, S], F32) for t in range(R)]
         gy = [sb("gy%d" % t, [P, S], F32) for t in range(R)]
         sig = [sb("sig%d" % t, [P, S], F32) for t in range(R)]
         gated = [sb("gated%d" % h, [P, R, HALF], F32) for h in range(2)]
         pulled = [sb("pulled%d" % h, [P, R, HALF], F32) for h in range(2)]
 
-        def scale_y(t):
-            nc.scalar.activation(gy[t][:], y_bank[t][:], ACT.Copy, scale=gain[:, t : t + 1])
-
-        def squash_d(t):
-            nc.scalar.activation(th[t][:], d_bank[t][:], ACT.Tanh, scale=0.5)
-            nc.gpsimd.tensor_scalar(sig[t][:], th[t][:], 0.5, 0.5, ALU.mult, ALU.add)
-
         def pull(t, h):
             nc.scalar.activation(pulled[h][:, t, :], gy[t][:].indirect(offsets(n1_l, half(h))), ACT.Copy, scale=-0.5)
 
         for t in range(R):
-            squash_d(t)
-        scale_y(0)
-        scale_y(1)
-        pull(0, 0)
-        scale_y(2)
-        pull(1, 0)
-        scale_y(3)
-        pull(2, 0)
-        pull(3, 0)
+            nc.scalar.activation(sig[t][:], d_bank[t][:], ACT.Sigmoid)
+        for t in range(R + 1):
+            if t < R:
+                nc.scalar.activation(gy[t][:], y_bank[t][:], ACT.Copy, scale=gain[:, t : t + 1])
+            if t > 0:
+                pull(t - 1, 0)
         for t in range(R):
             pull(t, 1)
 
-        def woven(ap, run):
-            return ap.rearrange("p (c i t) -> p c t i", i=run, t=R)
+        def woven(ap):
+            return ap.rearrange("p (c i t) -> p c t i", i=2, t=R)
 
-        def weave(ap, run):
-            return ap.rearrange("p t (c i) -> p c t i", i=run)
+        def weave(ap):
+            return ap.rearrange("p t (c i) -> p c t i", i=2)
 
         z16 = {}
         z_w = [sb("z_w%d" % h, [P, HALF], U32) for h in range(2)]
@@ -167,7 +159,7 @@ def tile_picked_twcgateblse_none_po_kernel(
 
         def combine(h):
             z16[h] = sb("z16", [P, HALF * R], BF16)
-            nc.vector.tensor_tensor(woven(z16[h][:], 2), weave(gated[h][:], 2), weave(pulled[h][:], 2), ALU.add)
+            nc.vector.tensor_tensor(woven(z16[h][:]), weave(gated[h][:]), weave(pulled[h][:]), ALU.add)
 
         def score(h):
             nc.vector.quantize_mx(z_w[h][:].bitcast(FP8X4), z_s[h][:], z16[h][:])
@@ -175,8 +167,8 @@ def tile_picked_twcgateblse_none_po_kernel(
                 bank = psum.tile([P, HALF], F32, name="bank%d" % (R * (1 - h) + t))
                 nc.tensor.matmul_mx(
                     bank[:],
-                    lhsT=cand_wd[:, P * t : P * (t + 1)].bitcast(FP8X4),
-                    lhsT_scale=cand_sd[:, P * t : P * (t + 1)],
+                    lhsT=cand_w[:, P * t : P * (t + 1)].bitcast(FP8X4),
+                    lhsT_scale=cand_s[:, P * t : P * (t + 1)],
                     rhs=z_w[h][:].bitcast(FP8X4),
                     rhs_scale=z_s[h][:],
                     start=True,
@@ -195,9 +187,7 @@ def tile_picked_twcgateblse_none_po_kernel(
         combine(1)
         score(1)
 
-        ON_VECTOR = 2
-        pieces = [slice(0, 256), slice(256, 384), slice(384, 512)]
-        widths = [cols.stop - cols.start for cols in pieces]
+        widths = [cols.stop - cols.start for cols in PIECES]
         ex = [sb("ex%d" % t, [P, S], F32) for t in range(R)]
         en = [sb("en%d" % t, [P, S], F32) for t in range(R)]
         ex_copy = [sb("ex_copy%d" % t, [P, S], F32) for t in range(ON_VECTOR)]
@@ -206,7 +196,7 @@ def tile_picked_twcgateblse_none_po_kernel(
         ratio = [sb("ratio%d" % k, [P, R, w], F32) for k, w in enumerate(widths)]
         o32 = [sb("o32_%d" % k, [P, R, w], F32) for k, w in enumerate(widths)]
         o16 = [sb("o16_%d" % k, [P, w * R], BF16) for k, w in enumerate(widths)]
-        o_w = [sb("o_w%d" % k, [P, w], U32) for k, w in enumerate(widths)]
+        o_w = sb("o_w", [P, S], U32)
         o_s = sb("o_s", [P, S], U8)
 
         def exp_up(t, h):
@@ -230,60 +220,54 @@ def tile_picked_twcgateblse_none_po_kernel(
                 nc.vector.tensor_tensor(total[:, t, half(h)], fetched[h][:, t - ON_VECTOR, :], ex[t][:, half(h)], ALU.add)
 
         def divide(t, k):
-            nc.vector.tensor_tensor(ratio[k][:, t, :], en[t][:].indirect(offsets(n4_l, pieces[k])), total[:, t, pieces[k]], ALU.mult)
+            nc.vector.tensor_tensor(ratio[k][:, t, :], en[t][:].indirect(offsets(n4_l, PIECES[k])), total[:, t, PIECES[k]], ALU.mult)
+
+        def add_and_divide(t, h):
+            add_pair(t, h)
+            add_pair(t + 1, h)
+            divide(t, h)
+            divide(t + 1, h)
 
         out_rows = out_0.rearrange("(p t) c -> p t c", t=R)
         out_words = out_1[0].rearrange("p c r -> p (c r)").bitcast(I32)
 
-        def planes(k):
-            nc.vector.quantize_mx(o_w[k][:].bitcast(FP8X4), o_s[:, pieces[k]], o16[k][:])
-            nc.sync.dma_start(out_words[:, pieces[k]], o_w[k][:].bitcast(I32))
+        def round_out(k):
+            nc.vector.tensor_copy(woven(o16[k][:]), weave(o32[k][:]))
 
-        exp_up(0, 0)
-        exp_up(1, 0)
-        exp_up(0, 1)
-        exp_up(1, 1)
-        exp_down(0, 0)
-        exp_down(0, 1)
-        exp_up(2, 0)
-        exp_up(2, 1)
-        exp_down(1, 0)
-        exp_down(1, 1)
-        exp_up(3, 0)
-        exp_up(3, 1)
-        fetch(2, 0)
-        exp_down(2, 0)
-        exp_down(2, 1)
-        fetch(3, 0)
-        exp_down(3, 0)
-        exp_down(3, 1)
+        def quantise_out(k):
+            nc.vector.quantize_mx(o_w[:, PIECES[k]].bitcast(FP8X4), o_s[:, PIECES[k]], o16[k][:])
 
-        for t in (0, 2):
-            add_pair(t, 0)
-            add_pair(t + 1, 0)
-            divide(t, 0)
-            divide(t + 1, 0)
+        for t in range(R + 1):
+            if t < R:
+                exp_up(t, 0)
+                exp_up(t, 1)
+            if t > ON_VECTOR:
+                fetch(t - 1, 0)
+            if t > 0:
+                exp_down(t - 1, 0)
+                exp_down(t - 1, 1)
+
+        add_and_divide(0, 0)
+        add_and_divide(2, 0)
         nc.scalar.activation(o32[0][:], ratio[0][:], ACT.Ln)
-        nc.sync.dma_start(out_rows[:, :, pieces[0]], o32[0][:])
-        fetch(2, 1)
-        fetch(3, 1)
-        nc.scalar.copy(woven(o16[0][:], 2), weave(o32[0][:], 2))
-        for t in (0, 2):
-            add_pair(t, 1)
-            add_pair(t + 1, 1)
-            divide(t, 1)
-            divide(t + 1, 1)
-        planes(0)
+        nc.sync.dma_start(out_rows[:, :, PIECES[0]], o32[0][:])
+        for t in range(ON_VECTOR, R):
+            fetch(t, 1)
+        add_and_divide(0, 1)
+        round_out(0)
+        add_and_divide(2, 1)
+        quantise_out(0)
         nc.scalar.activation(o32[1][:], ratio[1][:], ACT.Ln)
-        nc.sync.dma_start(out_rows[:, :, pieces[1]], o32[1][:])
+        nc.sync.dma_start(out_rows[:, :, PIECES[1]], o32[1][:])
         for t in range(R):
             divide(t, 2)
         for t in (0, 2):
             nc.scalar.activation(o32[2][:, t : t + 2, :], ratio[2][:, t : t + 2, :], ACT.Ln)
-        nc.sync.dma_start(out_rows[:, :, pieces[2]], o32[2][:])
-        for k in (1, 2):
-            nc.vector.tensor_copy(woven(o16[k][:], 2), weave(o32[k][:], 2))
-            planes(k)
-        for q in range(4):
-            engine = nc.sync if q % 2 else nc.scalar
-            engine.dma_start(out_2[0, 4 * q : 4 * q + 4, :].bitcast(I32), o_s[32 * q : 32 * q + 4, :].bitcast(I32))
+        nc.sync.dma_start(out_rows[:, :, PIECES[2]], o32[2][:])
+        for k, cols in ((1, slice(0, PIECES[1].stop)), (2, PIECES[2])):
+            round_out(k)
+            quantise_out(k)
+            nc.sync.dma_start(out_words[:, cols], o_w[:, cols].bitcast(I32))
+        for q in range(QUADRANTS):
+            queue = nc.sync if q % 2 else nc.scalar
+            queue.dma_start(out_2[0, 4 * q : 4 * q + 4, :].bitcast(I32), o_s[32 * q : 32 * q + 4, :].bitcast(I32))

from contextlib import ExitStack

import concourse.mybir as mybir

F32 = mybir.dt.float32
BF16 = mybir.dt.bfloat16
I32 = mybir.dt.int32
U32 = mybir.dt.uint32
U16 = mybir.dt.uint16
U8 = mybir.dt.uint8
FP8X4 = mybir.dt.float8_e4m3fn_x4
FP4X4 = mybir.dt.float4_e2m1fn_x4
ACT = mybir.ActivationFunctionType
ALU = mybir.AluOpType

P = 128
R = 4
T = 2048
S = 512
HALF = S // 2
QUADRANTS = 4
ON_VECTOR = 2
PIECES = [slice(0, 256), slice(256, 384), slice(384, 512)]
FLOPS = 3 * 2 * 512 * 512 * 512


def tile_picked_twcgateblse_none_po_kernel(
    tc, x_words, x_scales, w1_words, w1_scales, w2_words, w2_scales, gs, offs, two, n1, n2, cand, n3, n4, out_0, out_1, out_2
):
    nc = tc.nc
    with ExitStack() as ctx:
        lists = ctx.enter_context(tc.tile_pool(name="lists", bufs=1))
        keep = ctx.enter_context(tc.tile_pool(name="keep", bufs=1))
        psum = ctx.enter_context(tc.psum_pool(name="psum", bufs=1))

        def sb(name, shape, dtype):
            return keep.tile(shape, dtype, name=name, align_bytes=64)

        def load_list(name, src):
            tile = lists.tile([P, S // 16], U16, name=name)
            nc.sync.dma_start(tile[:], src)
            return tile

        def load_scales(tile, src):
            for q in range(QUADRANTS):
                nc.sync.dma_start(tile[32 * q : 32 * q + 4, :].bitcast(I32), src[0, 4 * q : 4 * q + 4, :].bitcast(I32))

        def half(h):
            return slice(h * HALF, (h + 1) * HALF)

        def offsets(lst, cols):
            return lst[:, cols.start // 16 : cols.stop // 16]

        xw = sb("xw", [P, T], U32)
        xs = sb("xs", [P, T], U8)
        w_raw = [sb("w%d_raw" % i, [P, 2 * S], U8) for i in range(2)]
        ws_raw = [sb("ws%d_raw" % i, [P, S], U8) for i in range(2)]
        ws_dealt = [sb("ws%d_dealt" % i, [P, S], U8) for i in range(2)]
        gain = sb("gain", [P, R], F32)

        nc.vector.memset(xs[:].bitcast(I32), 0)
        nc.vector.memset(ws_raw[1][:].bitcast(I32), 0)
        nc.vector.memset(ws_raw[0][:].bitcast(I32), 0)

        for i, words in ((1, w2_words), (0, w1_words)):
            nc.gpsimd.dma_start(w_raw[i][:].bitcast(I32), words[0].bitcast(I32))
        x_rows = x_words[0].rearrange("p c r -> p (c r)").bitcast(I32)
        nc.sync.dma_start(xw[:, : T // 2].bitcast(I32), x_rows[:, : T // 2])
        two_l = load_list("two_l", two)
        load_scales(xs, x_scales)
        nc.sync.dma_start(xw[:, T // 2 :].bitcast(I32), x_rows[:, T // 2 :])
        load_scales(ws_raw[1], w2_scales)
        offs_l = load_list("offs_l", offs)
        load_scales(ws_raw[0], w1_scales)
        nc.sync.dma_start(gain[:], gs.rearrange("(p t) o -> p (t o)", t=R))
        cand_l = load_list("cand_l", cand)
        n1_l = load_list("n1_l", n1)
        n2_l = load_list("n2_l", n2)
        n3_l = load_list("n3_l", n3)
        n4_l = load_list("n4_l", n4)

        def deal(ap):
            return ap.rearrange("p (m t) -> p t m", t=R)

        def dealt(ap):
            return ap.rearrange("p (t m) -> p t m", t=R)

        def gather_scales(name, lst):
            tile = sb(name, [P, S], U8)
            nc.vector.tensor_copy(tile[:], xs[:].indirect(lst[:]))
            return tile

        def gather_words(name, lst):
            tile = sb(name, [P, S], U32)
            nc.vector.tensor_copy(tile[:], xw[:].indirect(lst[:]))
            return tile

        w_dealt = [sb("w%d_dealt" % i, [P, 2 * S], U8) for i in range(2)]
        for i in (1, 0):
            nc.scalar.copy(dealt(w_dealt[i][:].bitcast(U16)), deal(w_raw[i][:].bitcast(U16)))
        two_s = gather_scales("two_s", two_l)
        two_w = gather_words("two_w", two_l)
        nc.vector.tensor_copy(dealt(ws_dealt[1][:]), deal(ws_raw[1][:]))
        offs_s = gather_scales("offs_s", offs_l)
        offs_w = gather_words("offs_w", offs_l)
        nc.vector.tensor_copy(dealt(ws_dealt[0][:]), deal(ws_raw[0][:]))
        cand_s = sb("cand_s", [P, S], U8)
        cand_w = sb("cand_w", [P, S], U32)
        nc.vector.tensor_copy(cand_s[:].rearrange("p (t m) -> p m t", t=R), xs[:].indirect(cand_l[:]))
        nc.vector.tensor_copy(cand_w[:].rearrange("p (t m) -> p m t", t=R), xw[:].indirect(cand_l[:]))

        def project(i, t, words, scales):
            bank = psum.tile([P, S], F32, name="bank%d" % (R * i + t))
            nc.tensor.matmul_mx(
                bank[:],
                lhsT=w_dealt[i][:, 2 * P * t : 2 * P * (t + 1)].bitcast(FP4X4),
                lhsT_scale=ws_dealt[i][:, P * t : P * (t + 1)],
                rhs=words[:].bitcast(FP8X4),
                rhs_scale=scales[:],
                start=True,
                stop=True,
            )
            return bank

        d_bank = [project(1, t, two_w, two_s) for t in range(R)]
        y_bank = [project(0, t, offs_w, offs_s) for t in range(R)]

        gy = [sb("gy%d" % t, [P, S], F32) for t in range(R)]
        sig = [sb("sig%d" % t, [P, S], F32) for t in range(R)]
        gated = [sb("gated%d" % h, [P, R, HALF], F32) for h in range(2)]
        pulled = [sb("pulled%d" % h, [P, R, HALF], F32) for h in range(2)]

        def pull(t, h):
            nc.scalar.activation(pulled[h][:, t, :], gy[t][:].indirect(offsets(n1_l, half(h))), ACT.Copy, scale=-0.5)

        for t in range(R):
            nc.scalar.activation(sig[t][:], d_bank[t][:], ACT.Sigmoid)
        for t in range(R + 1):
            if t < R:
                nc.scalar.activation(gy[t][:], y_bank[t][:], ACT.Copy, scale=gain[:, t : t + 1])
            if t > 0:
                pull(t - 1, 0)
        for t in range(R):
            pull(t, 1)

        def woven(ap):
            return ap.rearrange("p (c i t) -> p c t i", i=2, t=R)

        def weave(ap):
            return ap.rearrange("p t (c i) -> p c t i", i=2)

        z16 = {}
        z_w = [sb("z_w%d" % h, [P, HALF], U32) for h in range(2)]
        z_s = [sb("z_s%d" % h, [P, HALF], U8) for h in range(2)]
        s_bank = {}

        def gate(t, h):
            nc.vector.tensor_tensor(gated[h][:, t, :], sig[t][:].indirect(offsets(n2_l, half(h))), gy[t][:, half(h)], ALU.mult)

        def combine(h):
            z16[h] = sb("z16", [P, HALF * R], BF16)
            nc.vector.tensor_tensor(woven(z16[h][:]), weave(gated[h][:]), weave(pulled[h][:]), ALU.add)

        def score(h):
            nc.vector.quantize_mx(z_w[h][:].bitcast(FP8X4), z_s[h][:], z16[h][:])
            for t in range(R):
                bank = psum.tile([P, HALF], F32, name="bank%d" % (R * (1 - h) + t))
                nc.tensor.matmul_mx(
                    bank[:],
                    lhsT=cand_w[:, P * t : P * (t + 1)].bitcast(FP8X4),
                    lhsT_scale=cand_s[:, P * t : P * (t + 1)],
                    rhs=z_w[h][:].bitcast(FP8X4),
                    rhs_scale=z_s[h][:],
                    start=True,
                    stop=True,
                )
                s_bank[t, h] = bank

        for t in range(R):
            gate(t, 0)
        gate(0, 1)
        combine(0)
        gate(1, 1)
        score(0)
        gate(2, 1)
        gate(3, 1)
        combine(1)
        score(1)

        widths = [cols.stop - cols.start for cols in PIECES]
        ex = [sb("ex%d" % t, [P, S], F32) for t in range(R)]
        en = [sb("en%d" % t, [P, S], F32) for t in range(R)]
        ex_copy = [sb("ex_copy%d" % t, [P, S], F32) for t in range(ON_VECTOR)]
        fetched = [sb("fetched%d" % h, [P, R - ON_VECTOR, HALF], F32) for h in range(2)]
        total = sb("total", [P, R, S], F32)
        ratio = [sb("ratio%d" % k, [P, R, w], F32) for k, w in enumerate(widths)]
        o32 = [sb("o32_%d" % k, [P, R, w], F32) for k, w in enumerate(widths)]
        o16 = [sb("o16_%d" % k, [P, w * R], BF16) for k, w in enumerate(widths)]
        o_w = sb("o_w", [P, S], U32)
        o_s = sb("o_s", [P, S], U8)

        def exp_up(t, h):
            nc.scalar.activation(ex[t][:, half(h)], s_bank[t, h][:], ACT.Exp, scale=0.0625)
            if t < ON_VECTOR:
                if h == 0:
                    nc.vector.tensor_copy(ex_copy[t][:, half(h)], ex[t][:, half(h)])
                else:
                    nc.sync.dma_start(ex_copy[t][:, half(h)], ex[t][:, half(h)])

        def exp_down(t, h):
            nc.scalar.activation(en[t][:, half(h)], s_bank[t, h][:], ACT.Exp, scale=-0.0625)

        def fetch(t, h):
            nc.scalar.activation(fetched[h][:, t - ON_VECTOR, :], ex[t][:].indirect(offsets(n3_l, half(h))), ACT.Copy)

        def add_pair(t, h):
            if t < ON_VECTOR:
                nc.vector.tensor_tensor(total[:, t, half(h)], ex[t][:].indirect(offsets(n3_l, half(h))), ex_copy[t][:, half(h)], ALU.add)
            else:
                nc.vector.tensor_tensor(total[:, t, half(h)], fetched[h][:, t - ON_VECTOR, :], ex[t][:, half(h)], ALU.add)

        def divide(t, k):
            nc.vector.tensor_tensor(ratio[k][:, t, :], en[t][:].indirect(offsets(n4_l, PIECES[k])), total[:, t, PIECES[k]], ALU.mult)

        def add_and_divide(t, h):
            add_pair(t, h)
            add_pair(t + 1, h)
            divide(t, h)
            divide(t + 1, h)

        out_rows = out_0.rearrange("(p t) c -> p t c", t=R)
        out_words = out_1[0].rearrange("p c r -> p (c r)").bitcast(I32)

        def round_out(k):
            nc.vector.tensor_copy(woven(o16[k][:]), weave(o32[k][:]))

        def quantise_out(k):
            nc.vector.quantize_mx(o_w[:, PIECES[k]].bitcast(FP8X4), o_s[:, PIECES[k]], o16[k][:])

        for t in range(R + 1):
            if t < R:
                exp_up(t, 0)
                exp_up(t, 1)
            if t > ON_VECTOR:
                fetch(t - 1, 0)
            if t > 0:
                exp_down(t - 1, 0)
                exp_down(t - 1, 1)

        add_and_divide(0, 0)
        add_and_divide(2, 0)
        nc.scalar.activation(o32[0][:], ratio[0][:], ACT.Ln)
        nc.sync.dma_start(out_rows[:, :, PIECES[0]], o32[0][:])
        for t in range(ON_VECTOR, R):
            fetch(t, 1)
        add_and_divide(0, 1)
        round_out(0)
        add_and_divide(2, 1)
        quantise_out(0)
        nc.scalar.activation(o32[1][:], ratio[1][:], ACT.Ln)
        nc.sync.dma_start(out_rows[:, :, PIECES[1]], o32[1][:])
        for t in range(R):
            divide(t, 2)
        for t in (0, 2):
            nc.scalar.activation(o32[2][:, t : t + 2, :], ratio[2][:, t : t + 2, :], ACT.Ln)
        nc.sync.dma_start(out_rows[:, :, PIECES[2]], o32[2][:])
        for k, cols in ((1, slice(0, PIECES[1].stop)), (2, PIECES[2])):
            round_out(k)
            quantise_out(k)
            nc.sync.dma_start(out_words[:, cols], o_w[:, cols].bitcast(I32))
        for q in range(QUADRANTS):
            queue = nc.sync if q % 2 else nc.scalar
            queue.dma_start(out_2[0, 4 * q : 4 * q + 4, :].bitcast(I32), o_s[32 * q : 32 * q + 4, :].bitcast(I32))
